import numpy as np
CORES = [2,10,34,50,74,82,98,114,130,138,162,178,202,210,226,242]
N = 16
GR, GC = 2, 8
L, KA, KB, F = 8, 1, 4, 128
def setup_inputs(rng):
    return {"a": rng.standard_normal((N, 128, KA * 128), dtype=np.float32), "b": rng.standard_normal((N, 128, KB * F), dtype=np.float32)}
def reference(a, b):
    A, B = a.astype(np.float64), b.astype(np.float64)
    y = np.zeros((N, 128, F))
    for i in range(GR):
        for j in range(GC):
            for k in range(L):
                At = A[i * GC + k // KA][:, 128 * (k % KA):128 * (k % KA) + 128]
                Bt = B[(k // KB) * GC + j][:, F * (k % KB):F * (k % KB) + F]
                y[i * GC + j] += At.T @ Bt
    return {"y": y.astype(np.float32 if a.dtype != np.float64 else np.float64)}

@@ -1,0 +1,77 @@
+from concourse.bass import DstId, RemoteDMATransfer
+
+GR, GC, KB, P = 2, 8, 4, 128
+
+SCRATCH = {
+    "A": ("sbuf", [P, GC * P], "float32"),
+    "B": ("sbuf", [P, GR * KB * P], "float32"),
+    "acc": ("psum", [P, P], "float32"),
+    "out": ("sbuf", [P, P], "float32"),
+}
+SEMAPHORES = ["la", "lb", "sent", "rb", "mm", "cp", "st"] + ["ra%d" % k for k in range(GC)]
+
+FIRST = [1, 2, 3, 4]
+LAST = [5, 6, 7]
+
+
+def _bits(m):
+    return bin(m).count("1")
+
+
+def rank_program(g, core, T, topo):
+    rank = T.rank_of(core)
+    if rank is None:
+        return
+    sem = T.sem
+    i, j = rank // GC, rank % GC
+    a_sl = T.A[:, j * P:(j + 1) * P]
+    b_sl = T.B[:, i * KB * P:(i + 1) * KB * P]
+
+    g.sync.dma_start(a_sl, T.a[:]).then_inc(sem.la, 16)
+    g.scalar.dma_start(b_sl, T.b[:]).then_inc(sem.lb, 16)
+
+    def send_a(offsets):
+        dsts = [T.cores[i * GC + (j + o) % GC] for o in offsets]
+        m = topo.mask(core, dsts[0])
+        ids = []
+        for d in dsts:
+            m &= topo.mask(core, d)
+            rid, pid = topo.addr(d, core)
+            ids.append(DstId(rid=rid, pnc=pid))
+        g.remote_dma_fused([RemoteDMATransfer(dst_ids=ids, dma_engine_mask=m, remote_sem=sem["ra%d" % j],
+                                              srcs=[a_sl], dsts=[a_sl for _ in dsts], alu_op=0)], local_sem=sem.sent)
+        return _bits(m)
+
+    sent = 0
+    g.wait_ge(sem.la, 16)
+    sent += send_a(FIRST)
+    partner = T.cores[(1 - i) * GC + j]
+    rid, pid = topo.addr(partner, core)
+    mb = topo.mask(core, partner)
+    g.wait_ge(sem.lb, 16)
+    g.remote_dma(out_ap=b_sl, in_ap=b_sl, remote_sem=sem.rb, local_sem=sem.sent, pid=pid, routing_id=rid, dma_engine_mask=mb)
+    sent += _bits(mb)
+    sent += send_a(LAST)
+
+    early = [j] + [(j - o) % GC for o in FIRST]
+    order = [k for k in early if k // KB == i] + [k for k in early if k // KB != i] + [(j - o) % GC for o in LAST]
+    g.tensor.wait_ge(sem.la, 16)
+    g.tensor.wait_ge(sem.lb, 16)
+    have_rb = False
+    for n, k in enumerate(order):
+        if k != j:
+            src = T.cores[i * GC + k]
+            g.tensor.wait_ge(sem["ra%d" % k], _bits(topo.mask(src, core)))
+        if k // KB != i and not have_rb:
+            g.tensor.wait_ge(sem.rb, _bits(topo.mask(partner, core)))
+            have_rb = True
+        mm = g.tensor.matmul(T.acc[:], T.A[:, k * P:(k + 1) * P], T.B[:, k * P:(k + 1) * P],
+                             start=(n == 0), stop=(n == len(order) - 1))
+    mm.then_inc(sem.mm, 1)
+
+    g.vector.wait_ge(sem.mm, 1)
+    g.vector.tensor_copy(T.out[:], T.acc[:]).then_inc(sem.cp, 1)
+    g.sync.wait_ge(sem.cp, 1)
+    g.sync.dma_start(T.y[:], T.out[:]).then_inc(sem.st, 16)
+    g.sync.wait_ge(sem.st, 16)
+    g.wait_ge(sem.sent, sent)

@@ -1,6 +1,7 @@
 from concourse.bass import DstId, RemoteDMATransfer
 
 GR, GC, KB, P = 2, 8, 4, 128
+NCORES = 256
 
 SCRATCH = {
     "A": ("sbuf", [P, GC * P], "float32"),
@@ -8,65 +9,111 @@ SCRATCH = {
     "acc": ("psum", [P, P], "float32"),
     "out": ("sbuf", [P, P], "float32"),
 }
-SEMAPHORES = ["la", "lb", "sent", "rb", "mm", "cp", "st"] + ["ra%d" % k for k in range(GC)]
+SEMAPHORES = ["la", "lb", "sent", "ha", "rb", "mm", "cp", "st"] + ["ra%d" % k for k in range(GC)]
 
-FIRST = [1, 2, 3, 4]
-LAST = [5, 6, 7]
+PLAN = [([1], True, [2, 3, 4]), ([5, 6], False, []), ([7], False, [])]
+LAG = 5.0
 
 
 def _bits(m):
     return bin(m).count("1")
 
 
+def _team(owner, T, topo):
+    h = [c for c in range(NCORES)
+         if topo.host(c) == topo.host(owner) and topo.chip(c) == topo.chip(owner) and T.rank_of(c) is None
+         and all(topo.may_write(c, d) for d in T.cores)]
+    h.sort(key=lambda c: (topo.die(c) == topo.die(owner), c))
+    return [owner] + h[:len(PLAN) - 1]
+
+
+def _arrivals():
+    ta, tb = {0: 0.0}, 0.0
+    for s, (pre, with_b, post) in enumerate(PLAN):
+        t = LAG + 0.5 * (s - 1) if s else 0.5
+        for o in pre:
+            t += 1
+            ta[o] = t
+        if with_b:
+            t += KB
+            tb = t
+        for o in post:
+            t += 1
+            ta[o] = t
+    return ta, tb
+
+
 def rank_program(g, core, T, topo):
-    rank = T.rank_of(core)
-    if rank is None:
+    owner = None
+    for rc in T.cores:
+        if topo.host(rc) == topo.host(core) and topo.chip(rc) == topo.chip(core):
+            owner = rc
+    if owner is None:
         return
+    team = _team(owner, T, topo)
+    if core not in team:
+        return
+    s = team.index(core)
+    helpers = team[1:]
     sem = T.sem
+    rank = T.rank_of(owner)
     i, j = rank // GC, rank % GC
     a_sl = T.A[:, j * P:(j + 1) * P]
     b_sl = T.B[:, i * KB * P:(i + 1) * KB * P]
+    partner = T.cores[(1 - i) * GC + j]
+    pre, with_b, post = PLAN[s]
 
-    g.sync.dma_start(a_sl, T.a[:]).then_inc(sem.la, 16)
-    g.scalar.dma_start(b_sl, T.b[:]).then_inc(sem.lb, 16)
-
-    def send_a(offsets):
-        dsts = [T.cores[i * GC + (j + o) % GC] for o in offsets]
-        m = topo.mask(core, dsts[0])
+    def write(src, dsts, m, rsem):
         ids = []
         for d in dsts:
-            m &= topo.mask(core, d)
             rid, pid = topo.addr(d, core)
             ids.append(DstId(rid=rid, pnc=pid))
-        g.remote_dma_fused([RemoteDMATransfer(dst_ids=ids, dma_engine_mask=m, remote_sem=sem["ra%d" % j],
-                                              srcs=[a_sl], dsts=[a_sl for _ in dsts], alu_op=0)], local_sem=sem.sent)
+        g.remote_dma_fused([RemoteDMATransfer(dst_ids=ids, dma_engine_mask=m, remote_sem=rsem, srcs=[src],
+                                              dsts=[src for _ in dsts], alu_op=0)], local_sem=sem.sent)
         return _bits(m)
 
-    sent = 0
-    g.wait_ge(sem.la, 16)
-    sent += send_a(FIRST)
-    partner = T.cores[(1 - i) * GC + j]
-    rid, pid = topo.addr(partner, core)
-    mb = topo.mask(core, partner)
-    g.wait_ge(sem.lb, 16)
-    g.remote_dma(out_ap=b_sl, in_ap=b_sl, remote_sem=sem.rb, local_sem=sem.sent, pid=pid, routing_id=rid, dma_engine_mask=mb)
-    sent += _bits(mb)
-    sent += send_a(LAST)
+    def send_a(offsets):
+        if not offsets:
+            return 0
+        dsts = [T.cores[i * GC + (j + o) % GC] for o in offsets]
+        m = topo.mask(core, dsts[0])
+        for d in dsts:
+            m &= topo.mask(core, d)
+        return write(a_sl, dsts, m, sem["ra%d" % j])
 
-    early = [j] + [(j - o) % GC for o in FIRST]
-    order = [k for k in early if k // KB == i] + [k for k in early if k // KB != i] + [(j - o) % GC for o in LAST]
+    off = topo.mask(owner, partner)
+    feed = topo.mask(owner, helpers[0]) & ~off
+
+    sent = 0
+    if s == 0:
+        g.sync.dma_start(a_sl, T.a[:]).then_inc(sem.la, 16)
+        g.scalar.dma_start(b_sl, T.b[:]).then_inc(sem.lb, 16)
+        g.wait_ge(sem.la, 16)
+        sent += write(a_sl, helpers, feed, sem.ha)
+    else:
+        g.wait_ge(sem.ha, _bits(feed))
+    sent += send_a(pre)
+    if with_b:
+        g.wait_ge(sem.lb, 16)
+        sent += write(b_sl, [partner], off, sem.rb)
+    sent += send_a(post)
+    g.wait_ge(sem.sent, sent)
+    if s:
+        return
+
+    ta, tb = _arrivals()
+    ready = sorted((max(ta[(j - k) % GC], tb if k // KB != i else 0.0), k) for k in range(GC))
     g.tensor.wait_ge(sem.la, 16)
     g.tensor.wait_ge(sem.lb, 16)
     have_rb = False
-    for n, k in enumerate(order):
+    for n, (t, k) in enumerate(ready):
         if k != j:
-            src = T.cores[i * GC + k]
-            g.tensor.wait_ge(sem["ra%d" % k], _bits(topo.mask(src, core)))
+            g.tensor.wait_ge(sem["ra%d" % k], _bits(off))
         if k // KB != i and not have_rb:
-            g.tensor.wait_ge(sem.rb, _bits(topo.mask(partner, core)))
+            g.tensor.wait_ge(sem.rb, _bits(off))
             have_rb = True
         mm = g.tensor.matmul(T.acc[:], T.A[:, k * P:(k + 1) * P], T.B[:, k * P:(k + 1) * P],
-                             start=(n == 0), stop=(n == len(order) - 1))
+                             start=(n == 0), stop=(n == GC - 1))
     mm.then_inc(sem.mm, 1)
 
     g.vector.wait_ge(sem.mm, 1)
@@ -74,4 +121,3 @@ def rank_program(g, core, T, topo):
     g.sync.wait_ge(sem.cp, 1)
     g.sync.dma_start(T.y[:], T.out[:]).then_inc(sem.st, 16)
     g.sync.wait_ge(sem.st, 16)
-    g.wait_ge(sem.sent, sent)

from concourse.bass import DstId, RemoteDMATransfer

GR, GC, KB, P = 2, 8, 4, 128
NCORES = 256

SCRATCH = {
    "A": ("sbuf", [P, GC * P], "float32"),
    "B": ("sbuf", [P, GR * KB * P], "float32"),
    "acc": ("psum", [P, P], "float32"),
    "out": ("sbuf", [P, P], "float32"),
}
SEMAPHORES = ["la", "lb", "sent", "ha", "rb", "mm", "cp", "st"] + ["ra%d" % k for k in range(GC)]

PLAN = [([1], True, [2, 3, 4]), ([5, 6], False, []), ([7], False, [])]
LAG = 5.0


def _bits(m):
    return bin(m).count("1")


def _team(owner, T, topo):
    h = [c for c in range(NCORES)
         if topo.host(c) == topo.host(owner) and topo.chip(c) == topo.chip(owner) and T.rank_of(c) is None
         and all(topo.may_write(c, d) for d in T.cores)]
    h.sort(key=lambda c: (topo.die(c) == topo.die(owner), c))
    return [owner] + h[:len(PLAN) - 1]


def _arrivals():
    ta, tb = {0: 0.0}, 0.0
    for s, (pre, with_b, post) in enumerate(PLAN):
        t = LAG + 0.5 * (s - 1) if s else 0.5
        for o in pre:
            t += 1
            ta[o] = t
        if with_b:
            t += KB
            tb = t
        for o in post:
            t += 1
            ta[o] = t
    return ta, tb


def rank_program(g, core, T, topo):
    owner = None
    for rc in T.cores:
        if topo.host(rc) == topo.host(core) and topo.chip(rc) == topo.chip(core):
            owner = rc
    if owner is None:
        return
    team = _team(owner, T, topo)
    if core not in team:
        return
    s = team.index(core)
    helpers = team[1:]
    sem = T.sem
    rank = T.rank_of(owner)
    i, j = rank // GC, rank % GC
    a_sl = T.A[:, j * P:(j + 1) * P]
    b_sl = T.B[:, i * KB * P:(i + 1) * KB * P]
    partner = T.cores[(1 - i) * GC + j]
    pre, with_b, post = PLAN[s]

    def write(src, dsts, m, rsem):
        ids = []
        for d in dsts:
            rid, pid = topo.addr(d, core)
            ids.append(DstId(rid=rid, pnc=pid))
        g.remote_dma_fused([RemoteDMATransfer(dst_ids=ids, dma_engine_mask=m, remote_sem=rsem, srcs=[src],
                                              dsts=[src for _ in dsts], alu_op=0)], local_sem=sem.sent)
        return _bits(m)

    def send_a(offsets):
        if not offsets:
            return 0
        dsts = [T.cores[i * GC + (j + o) % GC] for o in offsets]
        m = topo.mask(core, dsts[0])
        for d in dsts:
            m &= topo.mask(core, d)
        return write(a_sl, dsts, m, sem["ra%d" % j])

    off = topo.mask(owner, partner)
    feed = topo.mask(owner, helpers[0]) & ~off

    sent = 0
    if s == 0:
        g.sync.dma_start(a_sl, T.a[:]).then_inc(sem.la, 16)
        g.scalar.dma_start(b_sl, T.b[:]).then_inc(sem.lb, 16)
        g.wait_ge(sem.la, 16)
        sent += write(a_sl, helpers, feed, sem.ha)
    else:
        g.wait_ge(sem.ha, _bits(feed))
    sent += send_a(pre)
    if with_b:
        g.wait_ge(sem.lb, 16)
        sent += write(b_sl, [partner], off, sem.rb)
    sent += send_a(post)
    g.wait_ge(sem.sent, sent)
    if s:
        return

    ta, tb = _arrivals()
    ready = sorted((max(ta[(j - k) % GC], tb if k // KB != i else 0.0), k) for k in range(GC))
    g.tensor.wait_ge(sem.la, 16)
    g.tensor.wait_ge(sem.lb, 16)
    have_rb = False
    for n, (t, k) in enumerate(ready):
        if k != j:
            g.tensor.wait_ge(sem["ra%d" % k], _bits(off))
        if k // KB != i and not have_rb:
            g.tensor.wait_ge(sem.rb, _bits(off))
            have_rb = True
        mm = g.tensor.matmul(T.acc[:], T.A[:, k * P:(k + 1) * P], T.B[:, k * P:(k + 1) * P],
                             start=(n == 0), stop=(n == GC - 1))
    mm.then_inc(sem.mm, 1)

    g.vector.wait_ge(sem.mm, 1)
    g.vector.tensor_copy(T.out[:], T.acc[:]).then_inc(sem.cp, 1)
    g.sync.wait_ge(sem.cp, 1)
    g.sync.dma_start(T.y[:], T.out[:]).then_inc(sem.st, 16)
    g.sync.wait_ge(sem.st, 16)
